import numpy as np
import ml_dtypes


def mxq(x, axis, fmt="e4m3"):
    dtype, down = {"e4m3": (ml_dtypes.float8_e4m3fn, 7), "e5m2": (ml_dtypes.float8_e5m2, 14)}[fmt]
    v = np.moveaxis(np.asarray(x, np.float32).astype(ml_dtypes.bfloat16).astype(np.float64), axis, -1)
    blocks = v.reshape(v.shape[:-1] + (-1, 32))
    amax = np.abs(blocks).max(-1, keepdims=True)
    byte = np.maximum(np.where(amax > 0, np.frexp(amax)[1] - 1 + 127, 0) - down, 1)
    scale = np.exp2(byte - 127.0)
    codes = (blocks / scale).astype(np.float32).astype(dtype).astype(np.float64)
    return np.moveaxis((codes * scale).reshape(v.shape), -1, axis)


WIDE = False


def mx_kscale(k):
    if not WIDE:
        return np.ones(k)
    levels = np.array([10, -10, 5, -5, 0])
    if k % 512:
        return np.exp2(np.random.permutation(np.resize(levels, k // 32))).repeat(32)
    a = np.empty((k // 512, 16))
    for p in range(k // 512):
        a[p, :8] = np.random.permutation(np.resize(levels, 8))
        for g in range(8):
            far = levels[np.abs(levels - a[p, g]) >= 10]
            a[p, g + 8] = far[np.random.randint(len(far))]
    return np.exp2(a.ravel()).repeat(32)


def f64(x):
    return np.asarray(x).astype(np.float64)


def striped(idx):
    return np.tile(np.asarray(idx).reshape(-1, 16).T, (8, 1)).astype(np.uint16)


def unstriped(offs):
    return offs[:16].T.reshape(-1).astype(np.int64)


def striped8(idx):
    return np.asarray(idx).reshape(8, -1, 16).transpose(0, 2, 1).reshape(128, -1).astype(np.uint16)


def unstriped8(offs):
    return offs.reshape(8, 16, -1).transpose(0, 2, 1).reshape(8, -1).astype(np.int64)


def pick8(x, idx, run):
    r = np.arange(len(x))
    return x[r[:, None], idx[r % (8 * run) // run]]


E2M1 = np.array([0.0, 0.5, 1.0, 1.5, 2.0, 3.0, 4.0, 6.0, -0.0, -0.5, -1.0, -1.5, -2.0, -3.0, -4.0, -6.0])


def pack_weight(w, fmt):
    k, n = w.shape
    w = f64(np.asarray(w, np.float32).astype(ml_dtypes.bfloat16)).reshape(k // 32, 32, n)
    amax = np.abs(w).max(1)
    if fmt == "e4m3":
        byte = np.frexp(amax)[1] - 1 + 127 - 7
    else:
        mant, ex = np.frexp(amax / 6.0)
        byte = np.where(mant > 0.5, ex, ex - 1) + 127
    byte = np.clip(np.where(amax > 0, byte, 1), 1, 254)
    scaled = (w * np.exp2(127.0 - byte)[:, None, :]).reshape(k, n).astype(np.float32)
    by_word = np.ascontiguousarray(scaled.reshape(k // 512, 128, 4, n).transpose(0, 1, 3, 2))
    if fmt == "e4m3":
        words = by_word.astype(ml_dtypes.float8_e4m3fn).view(np.uint8)
    else:
        c = by_word.astype(ml_dtypes.float4_e2m1fn).view(np.uint8) & 0xF
        words = (c[..., 0::2] | (c[..., 1::2] << 4)).reshape(k // 512, 128, 2 * n)
    return np.ascontiguousarray(words), np.ascontiguousarray(byte.astype(np.uint8).reshape(k // 512, 16, n))


def unpack_weight(words, scales, fmt):
    g, _, n = scales.shape
    words = np.ascontiguousarray(words).reshape(g, 128, n, -1)
    if fmt == "e4m3":
        vals = words.view(ml_dtypes.float8_e4m3fn).astype(np.float64)
    else:
        nib = np.empty((g, 128, n, 4), np.uint8)
        nib[..., 0::2] = words & 0xF
        nib[..., 1::2] = words >> 4
        vals = E2M1[nib]
    vals = vals * np.repeat(np.exp2(scales.astype(np.float64) - 127.0), 8, axis=1)[..., None]
    return vals.transpose(0, 1, 3, 2).reshape(g * 512, n)


K, J, R, T, Z, M, O, N, U, E, G = 512, 512, 512, 1024, 512, 1024, 256, 256, 512, 128, 256


def setup_inputs():
    n = np.random.standard_normal
    idx = np.random.permutation(T)[:J]
    idx2 = np.random.permutation(M)[:J]
    idx3 = np.stack([np.random.permutation(J)[:O] for _ in range(8)])
    idx4 = np.stack([np.random.permutation(U)[:O] for _ in range(8)])
    idx5 = np.stack([np.random.permutation(O)[:E] for _ in range(8)])
    idx6 = np.stack([np.random.permutation(G)[:E] for _ in range(8)])
    fk = mx_kscale(K)
    fr = mx_kscale(R)
    fz = mx_kscale(Z)
    xtp = pack_weight(n((K, T)) * fk[:, None], "e2m1")
    wp = pack_weight(n((K, R)) * 1 / np.sqrt(K) / fk[:, None] * fr, "e4m3")
    xop = pack_weight(n((Z, M)) / fz[:, None], "e2m1")
    w2p = pack_weight(n((Z, R)) * 1 / np.sqrt(Z) * fz[:, None] * fr, "e4m3")
    wbp = pack_weight(n((R, N)) * 1 / np.sqrt(R) / fr[:, None], "e4m3")
    wop = pack_weight(n((R, N)) * 1 / np.sqrt(R) / fr[:, None], "e2m1")
    return {
        "xt_words": xtp[0],
        "xt_scales": xtp[1],
        "w_words": wp[0],
        "w_scales": wp[1],
        "xo_words": xop[0],
        "xo_scales": xop[1],
        "w2_words": w2p[0],
        "w2_scales": w2p[1],
        "sa": (np.random.uniform(0.5, 1.6, (R, 1))).astype(np.float32),
        "wb_words": wbp[0],
        "wb_scales": wbp[1],
        "wo_words": wop[0],
        "wo_scales": wop[1],
        "se": (np.random.uniform(0.5, 1.6, (N, 1))).astype(np.float32),
        "offs": striped(idx),
        "offs2": striped(idx2),
        "offs3": striped8(idx3),
        "offs4": striped8(idx4),
        "offs5": striped8(idx5),
        "offs6": striped8(idx6),
    }


def reference(xt_words, xt_scales, w_words, w_scales, xo_words, xo_scales, w2_words, w2_scales, sa, wb_words, wb_scales, wo_words, wo_scales, se, offs, offs2, offs3, offs4, offs5, offs6):
    idx = unstriped(offs)
    idx2 = unstriped(offs2)
    idx3 = unstriped8(offs3)
    idx4 = unstriped8(offs4)
    idx5 = unstriped8(offs5)
    idx6 = unstriped8(offs6)
    xtu = unpack_weight(xt_words, xt_scales, "e2m1")
    wu = unpack_weight(w_words, w_scales, "e4m3")
    xou = unpack_weight(xo_words, xo_scales, "e2m1")
    w2u = unpack_weight(w2_words, w2_scales, "e4m3")
    wbu = unpack_weight(wb_words, wb_scales, "e4m3")
    wou = unpack_weight(wo_words, wo_scales, "e2m1")
    xtidxg = xtu[:, idx]
    xoidx2g = xou[:, idx2]
    a = wu.T @ xtidxg + w2u.T @ xoidx2g
    g1 = np.maximum(a, 0.0)
    hid = pick8(g1, idx3, 64) * f64(sa)
    hidq = mxq(hid, 0, "e4m3")
    p = wbu.T @ hidq
    q = wou.T @ hidq
    m0 = np.zeros((N, U))
    m0[np.arange(N)[:, None], idx4[np.arange(N) % 128 // 16]] = p
    m1 = pick8(q, idx5, 16) * f64(se)
    m2 = np.zeros((N, G))
    m2[np.arange(N)[:, None], idx6[np.arange(N) % 128 // 16]] = m1
    m3 = np.repeat(m2, U // G, axis=1)
    y = m0 - m3
    return y

from contextlib import ExitStack

import concourse.mybir as mybir

K, J, R, T, N, O, U, E, G = 512, 512, 512, 1024, 256, 256, 512, 128, 256
FLOPS = 2 * (2 * K * R * J + 2 * R * N * O)

F32 = mybir.dt.float32
BF16 = mybir.dt.bfloat16
I32 = mybir.dt.int32
U32 = mybir.dt.uint32
U16 = mybir.dt.uint16
U8 = mybir.dt.uint8
FP8X4 = mybir.dt.float8_e4m3fn_x4
FP4X4 = mybir.dt.float4_e2m1fn_x4
ACT = mybir.ActivationFunctionType

P = 128
PACK = 4
JH = J // 2
OH = O // 2
OQ = OH // 2


def tile_picked_tokens_plain_bank_kept_outcomes_endcoarse_kernel(
    tc, xt_words, xt_scales, w_words, w_scales, xo_words, xo_scales, w2_words, w2_scales, sa,
    wb_words, wb_scales, wo_words, wo_scales, se, offs, offs2, offs3, offs4, offs5, offs6, out,
):
    nc = tc.nc
    with ExitStack() as ctx:
        sb = ctx.enter_context(tc.tile_pool(name="sb", bufs=1))
        psum = ctx.enter_context(tc.psum_pool(name="psum", bufs=1))

        def sbuf(name, shape, dtype):
            return sb.tile(shape, dtype, name=name, align_bytes=64)

        def load_list(name, src):
            lst = sbuf(name, list(src.shape), U16)
            nc.sync.dma_start(lst[:], src)
            return lst

        def load_words(name, src, dtype, cols):
            words = sbuf(name, [P, cols], dtype)
            nc.sync.dma_start(words[:].bitcast(I32), src.bitcast(I32))
            return words

        def zero_plane(name, cols):
            plane = sbuf(name, [P, cols], U8)
            nc.vector.memset(plane[:].bitcast(I32), 0)
            return plane

        def load_scales(queue, plane, src):
            for quad in range(4):
                queue.dma_start(plane[32 * quad : 32 * quad + 4, :].bitcast(I32), src[0, 4 * quad : 4 * quad + 4, :].bitcast(I32))

        def e4m3_rows(src):
            return src[0].rearrange("p n t -> p (n t)")

        xt_plane = zero_plane("xt_plane", T)
        w_plane = zero_plane("w_plane", R)
        w2_plane = zero_plane("w2_plane", R)
        xo_plane = zero_plane("xo_plane", T)
        wb_plane = zero_plane("wb_plane", N)
        wo_plane = zero_plane("wo_plane", N)

        idx = load_list("idx", offs)
        xt_table = load_words("xt_table", xt_words[0], U16, T)
        load_scales(nc.sync, xt_plane, xt_scales)
        w_raw = load_words("w_raw", e4m3_rows(w_words), U32, R)
        load_scales(nc.sync, w_plane, w_scales)
        idx2 = load_list("idx2", offs2)
        xo_table = load_words("xo_table", xo_words[0], U16, T)
        load_scales(nc.sync, xo_plane, xo_scales)
        w2_raw = load_words("w2_raw", e4m3_rows(w2_words), U32, R)
        load_scales(nc.sync, w2_plane, w2_scales)
        idx3 = load_list("idx3", offs3)
        sa_cols = sbuf("sa_cols", [P, PACK], F32)
        nc.sync.dma_start(sa_cols[:], sa.rearrange("(p t) o -> p (t o)", t=PACK))
        wb_codes = load_words("wb_codes", e4m3_rows(wb_words), U32, N)
        load_scales(nc.sync, wb_plane, wb_scales)
        idx4 = load_list("idx4", offs4)
        wo_codes = load_words("wo_codes", wo_words[0], U16, N)
        load_scales(nc.sync, wo_plane, wo_scales)
        idx5 = load_list("idx5", offs5)
        idx6 = load_list("idx6", offs6)
        se_cols = sbuf("se_cols", [P, N // P], F32)
        with nc.allow_non_contiguous_dma(reason="one weight a partition for each tile of output features"):
            nc.sync.dma_start(se_cols[:], se.rearrange("(c p) o -> p (c o)", p=P))

        floor = sbuf("floor", [P, 1], F32)
        nc.vector.memset(floor[:], 0.0)
        fine = [sbuf("fine%d" % c, [P, U], F32) for c in range(N // P)]
        coarse = [sbuf("coarse%d" % c, [P, G], F32) for c in range(N // P)]
        for page in fine + coarse:
            nc.vector.memset(page[:], 0.0)

        def deal(name, raw, plane):
            codes = sbuf(name + "_codes", [P, PACK, P], U32)
            nc.scalar.copy(
                codes[:].rearrange("p t (b i) -> p b t i", i=4),
                raw[:].rearrange("p (b i t) -> p b t i", i=4, t=PACK),
            )
            scales = sbuf(name + "_dealt_plane", [P, PACK, P], U8)
            nc.vector.tensor_copy(scales[:], plane[:].rearrange("p (m t) -> p t m", t=PACK))
            return codes, scales

        def gather(name, table, lst, start, count, dtype):
            picked = sbuf(name, [P, count], dtype)
            nc.vector.tensor_copy(picked[:], table[:].indirect(lst[:, start // 16 : (start + count) // 16]))
            return picked

        xt_picked = gather("xt_picked", xt_table, idx, 0, J, U16)
        w_codes, w_dealt = deal("w", w_raw, w_plane)
        banks = {}
        for half in range(2):
            xt_picked_plane = gather("xt_picked_plane%d" % half, xt_plane, idx, half * JH, JH, U8)
            for t in range(PACK):
                banks[half, t] = psum.tile([P, JH], F32, name="a%d_%d" % (half, t), tag="bank%d" % (half * PACK + t))
                nc.tensor.matmul_mx(
                    banks[half, t][:], lhsT=w_codes[:, t, :].bitcast(FP8X4), lhsT_scale=w_dealt[:, t, :],
                    rhs=xt_picked[:, half * JH : (half + 1) * JH].bitcast(FP4X4), rhs_scale=xt_picked_plane[:],
                    start=True, stop=False,
                )

        w2_codes, w2_dealt = deal("w2", w2_raw, w2_plane)
        g1 = [sbuf("g1_%d" % t, [P, J], F32) for t in range(PACK)]
        for half in range(2):
            xo_picked = gather("xo_picked%d" % half, xo_table, idx2, half * JH, JH, U16)
            xo_picked_plane = gather("xo_picked_plane%d" % half, xo_plane, idx2, half * JH, JH, U8)
            for t in range(PACK):
                nc.tensor.matmul_mx(
                    banks[half, t][:], lhsT=w2_codes[:, t, :].bitcast(FP8X4), lhsT_scale=w2_dealt[:, t, :],
                    rhs=xo_picked[:].bitcast(FP4X4), rhs_scale=xo_picked_plane[:],
                    start=False, stop=True,
                )
        for t in range(PACK):
            nc.scalar.activation(g1[t][:, :JH], banks[0, t][:], ACT.Relu)
        for t in range(PACK):
            nc.vector.tensor_scalar_max(g1[t][:, JH:], banks[1, t][:], floor[:])

        hid = [sbuf("hid0", [P, PACK, OH], BF16), sb.tile([P, PACK, OH], BF16, name="hid1", tag="floor", align_bytes=64)]
        for half in range(2):
            for t in range(PACK):
                nc.scalar.activation(
                    hid[half][:, t, :], g1[t][:].indirect(idx3[:, half * OH // 16 : (half + 1) * OH // 16]),
                    ACT.Copy, scale=sa_cols[:, t : t + 1],
                )

        q_rows = [sbuf("q_rows%d" % c, [P, O], F32) for c in range(N // P)]
        for half in range(2):
            hid_codes = sbuf("hid_codes%d" % half, [P, OH], U32)
            hid_plane = sbuf("hid_plane%d" % half, [P, OH], U8)
            grouped = [sbuf("grouped%d" % s, [P, OQ * PACK], BF16) for s in range(2)]
            for s in range(2):
                nc.vector.tensor_copy(
                    grouped[s][:].rearrange("p (b i t) -> p b t i", i=4, t=PACK),
                    hid[half][:, :, s * OQ : (s + 1) * OQ].rearrange("p t (b i) -> p b t i", i=4),
                )
            for s in range(2):
                nc.vector.quantize_mx(
                    hid_codes[:, s * OQ : (s + 1) * OQ].bitcast(FP8X4), hid_plane[:, s * OQ : (s + 1) * OQ], grouped[s][:]
                )
            for c in range(N // P):
                p_bank = psum.tile([P, OH], F32, name="p%d_%d" % (half, c), tag="bank%d" % (half * PACK + c))
                nc.tensor.matmul_mx(
                    p_bank[:], lhsT=wb_codes[:, c * P : (c + 1) * P].bitcast(FP8X4), lhsT_scale=wb_plane[:, c * P : (c + 1) * P],
                    rhs=hid_codes[:].bitcast(FP8X4), rhs_scale=hid_plane[:], start=True, stop=True,
                )
                p_rows = sbuf("p_rows%d_%d" % (half, c), [P, OH], F32)
                (nc.scalar.copy if half == 0 else nc.vector.tensor_copy)(p_rows[:], p_bank[:])
                nc.scalar.activation(fine[c][:].indirect(idx4[:, half * OH // 16 : (half + 1) * OH // 16]), p_rows[:], ACT.Copy)
            for c in range(N // P):
                q_bank = psum.tile([P, OH], F32, name="q%d_%d" % (half, c), tag="bank%d" % (half * PACK + 2 + c))
                nc.tensor.matmul_mx(
                    q_bank[:], lhsT=wo_codes[:, c * P : (c + 1) * P].bitcast(FP4X4), lhsT_scale=wo_plane[:, c * P : (c + 1) * P],
                    rhs=hid_codes[:].bitcast(FP8X4), rhs_scale=hid_plane[:], start=True, stop=True,
                )
                nc.vector.tensor_copy(q_rows[c][:, half * OH : (half + 1) * OH], q_bank[:])

        m1 = [sbuf("m1_%d" % c, [P, E], F32) for c in range(N // P)]
        for c in range(N // P):
            nc.scalar.activation(m1[c][:], q_rows[c][:].indirect(idx5[:]), ACT.Copy, scale=se_cols[:, c : c + 1])
        for c in range(N // P):
            nc.scalar.activation(coarse[c][:].indirect(idx6[:]), m1[c][:], ACT.Copy)
            result = sbuf("result%d" % c, [P, G, U // G], F32)
            nc.vector.tensor_sub(
                result[:], fine[c][:].rearrange("p (g d) -> p g d", d=U // G),
                coarse[c][:].unsqueeze(2).to_broadcast([P, G, U // G]),
            )
            nc.sync.dma_start(out[c * P : (c + 1) * P, :], result[:].rearrange("p g d -> p (g d)"))
